import numpy as np
import ml_dtypes


def mxq(x, axis, fmt="e4m3"):
    dtype, down = {"e4m3": (ml_dtypes.float8_e4m3fn, 7), "e5m2": (ml_dtypes.float8_e5m2, 14)}[fmt]
    v = np.moveaxis(np.asarray(x, np.float32).astype(ml_dtypes.bfloat16).astype(np.float64), axis, -1)
    blocks = v.reshape(v.shape[:-1] + (-1, 32))
    amax = np.abs(blocks).max(-1, keepdims=True)
    byte = np.maximum(np.where(amax > 0, np.frexp(amax)[1] - 1 + 127, 0) - down, 1)
    scale = np.exp2(byte - 127.0)
    codes = (blocks / scale).astype(np.float32).astype(dtype).astype(np.float64)
    return np.moveaxis((codes * scale).reshape(v.shape), -1, axis)


WIDE = False


def mx_kscale(k):
    if not WIDE:
        return np.ones(k)
    levels = np.array([10, -10, 5, -5, 0])
    if k % 512:
        return np.exp2(np.random.permutation(np.resize(levels, k // 32))).repeat(32)
    a = np.empty((k // 512, 16))
    for p in range(k // 512):
        a[p, :8] = np.random.permutation(np.resize(levels, 8))
        for g in range(8):
            far = levels[np.abs(levels - a[p, g]) >= 10]
            a[p, g + 8] = far[np.random.randint(len(far))]
    return np.exp2(a.ravel()).repeat(32)


BF16 = ml_dtypes.bfloat16


def bf(x):
    return np.asarray(x, np.float32).astype(BF16)


def f64(x):
    return np.asarray(x).astype(np.float64)


E2M1 = np.array([0.0, 0.5, 1.0, 1.5, 2.0, 3.0, 4.0, 6.0, -0.0, -0.5, -1.0, -1.5, -2.0, -3.0, -4.0, -6.0])


def pack_weight(w, fmt):
    k, n = w.shape
    w = f64(bf(w)).reshape(k // 32, 32, n)
    amax = np.abs(w).max(1)
    if fmt == "e4m3":
        byte = np.frexp(amax)[1] - 1 + 127 - 7
    else:
        mant, ex = np.frexp(amax / 6.0)
        byte = np.where(mant > 0.5, ex, ex - 1) + 127
    byte = np.clip(np.where(amax > 0, byte, 1), 1, 254)
    scaled = (w * np.exp2(127.0 - byte)[:, None, :]).reshape(k, n).astype(np.float32)
    by_word = np.ascontiguousarray(scaled.reshape(k // 512, 128, 4, n).transpose(0, 1, 3, 2))
    if fmt == "e4m3":
        words = by_word.astype(ml_dtypes.float8_e4m3fn).view(np.uint8)
    else:
        c = by_word.astype(ml_dtypes.float4_e2m1fn).view(np.uint8) & 0xF
        words = c[..., 0::2] | (c[..., 1::2] << 4)
    return np.ascontiguousarray(words), np.ascontiguousarray(byte.astype(np.uint8).reshape(k // 512, 16, n))


def unpack_weight(words, scales, fmt):
    g, p, n, _ = words.shape
    if fmt == "e4m3":
        vals = np.ascontiguousarray(words).view(ml_dtypes.float8_e4m3fn).astype(np.float64)
    else:
        nib = np.empty((g, p, n, 4), np.uint8)
        nib[..., 0::2] = words & 0xF
        nib[..., 1::2] = words >> 4
        vals = E2M1[nib]
    vals = vals * np.repeat(np.exp2(scales.astype(np.float64) - 127.0), 8, axis=1)[..., None]
    return vals.transpose(0, 1, 3, 2).reshape(g * 512, n)
def pack4(w):
    words, scales = pack_weight(w, "e2m1")
    return words.reshape(words.shape[0], 128, -1), scales


def unpack4(words, scales):
    return unpack_weight(words.reshape(words.shape[0], 128, -1, 2), scales, "e2m1")


def planes(Y):
    n, m = Y.shape
    b = f64(bf(Y)).reshape(n // 32, 32, m)
    amax = np.abs(b).max(1)
    byte = np.clip(np.where(amax > 0, np.frexp(amax)[1] - 1 + 127 - 7, 1), 1, 254)
    codes = (b * np.exp2(127.0 - byte)[:, None, :]).reshape(n, m).astype(np.float32).astype(ml_dtypes.float8_e4m3fn).view(np.uint8)
    words = codes.reshape(n // 512, 128, 4, m).transpose(0, 1, 3, 2)
    return np.ascontiguousarray(words), np.ascontiguousarray(byte.astype(np.uint8).reshape(n // 512, 16, m))


M, E, KI, KB = 1024, 2048, 1024, 512

CUT = 0.5


def incidence(nodes, edges):
    w = np.random.randn(nodes, edges)
    return w * (np.abs(w) > CUT) / np.sqrt(nodes)


def setup_inputs():
    si = mx_kscale(KI)
    sb = mx_kscale(KB)
    a_words, a_scales = pack4(incidence(KI, E) * si[:, None])
    return {
        "a_words": a_words,
        "a_scales": a_scales,
        "v_int": bf(np.random.randn(KI, M) / si[:, None]),
        "d_inc": bf(incidence(KB, E) * sb[:, None]),
        "v_bnd": bf(np.random.randn(KB, M) / sb[:, None]),
        "emf": bf(0.4 * np.random.randn(E)),
        "cond": bf(np.exp(0.8 * np.random.randn(E))),
    }


def reference(a_words, a_scales, v_int, d_inc, v_bnd, emf, cond):
    A = unpack4(a_words, a_scales)
    drop_int = A.T @ mxq(f64(v_int), 0, "e4m3")
    drop_bnd = mxq(f64(d_inc), 0, "e4m3").T @ mxq(f64(v_bnd), 0, "e4m3")
    y = f64(cond)[:, None] * (drop_int + drop_bnd + f64(emf)[:, None])
    Y = y
    words, scales = planes(Y)
    return y, words, scales

@@ -1,0 +1,322 @@
+from contextlib import ExitStack
+
+import concourse.mybir as mybir
+
+F32 = mybir.dt.float32
+BF16 = mybir.dt.bfloat16
+I32 = mybir.dt.int32
+U32 = mybir.dt.uint32
+U8 = mybir.dt.uint8
+FP8X4 = mybir.dt.float8_e4m3fn_x4
+FP4X4 = mybir.dt.float4_e2m1fn_x4
+IDENTITY = mybir.ActivationFunctionType.Identity
+
+M, E, KI, KB = 1024, 2048, 1024, 512
+FLOPS = 2 * E * M * (KI + KB)
+
+P = 128
+PACK = 4
+W = 512
+GROUPS = E // W
+HALVES = M // W
+INT_PASSES = KI // W
+SHARE = 48
+BLOCKS = [(0, 0), (1, 0), (0, 1), (1, 1), (2, 0), (2, 1), (3, 0), (3, 1)]
+
+
+def tile_hypergraph_edge_flows_g5_kernel(
+    tc, a_words, a_scales, v_int, d_inc, v_bnd, emf, cond, out_0, out_1, out_2
+):
+    nc = tc.nc
+    with ExitStack() as ctx:
+        keep = ctx.enter_context(tc.tile_pool(name="keep", bufs=1))
+        stage = ctx.enter_context(tc.tile_pool(name="stage", bufs=4))
+        psum = ctx.enter_context(tc.psum_pool(name="psum", bufs=1))
+        ctx.enter_context(tc.manual_schedule())
+
+        raw = {}
+        grouped = {}
+        quant = {}
+        a_codes = {}
+        a_planes = {}
+        banks = {}
+        flows = {}
+        rounded = {}
+        out_codes = {}
+
+        def source(key):
+            kind, i, j = key
+            if kind == "vi":
+                rows = v_int[i * W : (i + 1) * W, j * W : (j + 1) * W]
+            elif kind == "vb":
+                rows = v_bnd[:, j * W : (j + 1) * W]
+            else:
+                rows = d_inc[:, j * W : (j + 1) * W]
+            return rows.rearrange("(p j) w -> p j w", j=PACK)
+
+        def load(key):
+            raw[key] = keep.tile([P, PACK, W], BF16, name="raw_%s_%d_%d" % key, align_bytes=64)
+            nc.sync.dma_start(out=raw[key][:], in_=source(key))
+
+        def load_a_words(pair, g):
+            raw[("a", pair, g)] = keep.tile([P, 4 * W], U8, name="a_raw_%d_%d" % (pair, g), align_bytes=64)
+            words = a_words.bitcast(I32)[g, :, pair * W : (pair + 1) * W]
+            nc.sync.dma_start(out=raw[("a", pair, g)][:].bitcast(I32), in_=words)
+
+        def load_a_scales(pair):
+            rows = a_scales.bitcast(I32).rearrange("g (q r) w -> r q g w", r=4)
+            for r in range(4):
+                nc.sync.dma_start(
+                    out=a_scale_rows[pair][r:P:32, :, :].bitcast(I32),
+                    in_=rows[r, :, :, pair * W // 2 : (pair + 1) * W // 2],
+                )
+
+        def copy_on(engine, out, in_):
+            if engine == "vector":
+                nc.vector.tensor_copy(out=out, in_=in_)
+            else:
+                nc.scalar.copy(out=out, in_=in_)
+
+        def interleave(key, engine, c0=0, c1=P):
+            if key not in grouped:
+                grouped[key] = stage.tile([P, PACK * W], BF16, name="grouped", align_bytes=64)
+            if key[0] == "d":
+                out = grouped[key][:].rearrange("p (t m j) -> p m j t", t=PACK, j=PACK)
+                in_ = raw[key][:].rearrange("p j (m t) -> p m j t", t=PACK)
+            else:
+                out = grouped[key][:].rearrange("p (c i j) -> p c j i", i=PACK, j=PACK)
+                in_ = raw[key][:].rearrange("p j (c i) -> p c j i", i=PACK)
+            copy_on(engine, out[:, c0:c1], in_[:, c0:c1])
+
+        def quantize(key):
+            codes = keep.tile([P, W], U32, name="codes_%s_%d_%d" % key, align_bytes=64)
+            plane = keep.tile([P, W], U8, name="plane_%s_%d_%d" % key, align_bytes=64)
+            nc.vector.quantize_mx(out=codes[:].bitcast(FP8X4), scales=plane[:], in_=grouped[key][:])
+            quant[key] = (codes, plane)
+
+        def sort_a_codes(e, g):
+            tile = keep.tile([P, PACK, 2 * P], U8, name="a_codes_%d_%d" % (e, g), align_bytes=64)
+            a_codes[(e, g)] = tile
+            words = raw[("a", e // 2, g)][:, e % 2 * 2 * W : (e % 2 + 1) * 2 * W]
+            nc.vector.tensor_copy(
+                out=tile[:].rearrange("p t (m b) -> p t m b", b=2),
+                in_=words.rearrange("p (m t b) -> p t m b", t=PACK, b=2),
+            )
+
+        def sort_a_scales(e, g):
+            tile = keep.tile([P, PACK, P], U8, name="a_plane_%d_%d" % (e, g), align_bytes=64)
+            a_planes[(e, g)] = tile
+            rows = a_scale_rows[e // 2][:, g, e % 2 * W : (e % 2 + 1) * W]
+            nc.vector.tensor_copy(out=tile[:], in_=rows.rearrange("p (m t) -> p t m", t=PACK))
+
+        def sort_a(e, g):
+            sort_a_codes(e, g)
+            sort_a_scales(e, g)
+
+        def multiply(e, h, t, which, start, stop):
+            if start:
+                bank = BLOCKS.index((e, h)) % 2 * PACK + t
+                banks[(e, h, t)] = psum.tile([P, W], F32, name="bank_%d" % bank)
+            if which == "b":
+                codes, plane = quant[("d", 0, e)]
+                lhs = codes[:, t * P : (t + 1) * P].bitcast(FP8X4)
+                lhs_scale = plane[:, t * P : (t + 1) * P]
+                codes, plane = quant[("vb", 0, h)]
+            else:
+                lhs = a_codes[(e, which)][:, t, :].bitcast(FP4X4)
+                lhs_scale = a_planes[(e, which)][:, t, :]
+                codes, plane = quant[("vi", which, h)]
+            nc.tensor.matmul_mx(
+                out=banks[(e, h, t)][:],
+                lhsT=lhs,
+                lhsT_scale=lhs_scale,
+                rhs=codes[:].bitcast(FP8X4),
+                rhs_scale=plane[:],
+                start=start,
+                stop=stop,
+            )
+
+        def multiply_pass(e, h, order, n):
+            for t in range(PACK):
+                multiply(e, h, t, order[n], n == 0, n == len(order) - 1)
+
+        def multiply_block(e, h):
+            for t in range(PACK):
+                for n, which in enumerate([0, 1, "b"]):
+                    multiply(e, h, t, which, n == 0, n == 2)
+
+        def empty_bank(e, h, t):
+            if t == 0:
+                flows[(e, h)] = keep.tile([P, PACK, W], F32, name="flow_%d_%d" % (e, h), align_bytes=64)
+            col = PACK * e + t
+            nc.scalar.activation(
+                out=flows[(e, h)][:, t, :],
+                in_=banks[(e, h, t)][:],
+                func=IDENTITY,
+                bias=source_term[:, col : col + 1],
+                scale=gain[:, col : col + 1],
+            )
+
+        def store_flow(e, h, t0, t1):
+            rows = out_0[e * W : (e + 1) * W, h * W : (h + 1) * W].rearrange("(p t) m -> p t m", t=PACK)
+            nc.sync.dma_start(out=rows[:, t0:t1, :], in_=flows[(e, h)][:, t0:t1, :])
+
+        def empty_block(e, h, step):
+            for t in range(PACK):
+                empty_bank(e, h, t)
+                if (t + 1) % step == 0:
+                    store_flow(e, h, t + 1 - step, t + 1)
+
+        def round_flow(e, h, engine, c0=0, c1=P):
+            if (e, h) not in rounded:
+                rounded[(e, h)] = stage.tile([P, PACK * W], BF16, name="rounded", align_bytes=64)
+            copy_on(
+                engine,
+                rounded[(e, h)][:].rearrange("p (c i t) -> p c t i", i=PACK, t=PACK)[:, c0:c1],
+                flows[(e, h)][:].rearrange("p t (c i) -> p c t i", i=PACK)[:, c0:c1],
+            )
+
+        def quantize_flow(e, h):
+            out_codes[(e, h)] = keep.tile([P, W], U32, name="out_codes_%d_%d" % (e, h), align_bytes=64)
+            nc.vector.quantize_mx(
+                out=out_codes[(e, h)][:].bitcast(FP8X4),
+                scales=out_planes[PACK * e : P, h * W : (h + 1) * W],
+                in_=rounded[(e, h)][:],
+            )
+
+        def store_codes(e, h):
+            words = out_1[e].rearrange("p m t -> p (m t)").bitcast(I32)
+            nc.sync.dma_start(out=words[:, h * W : (h + 1) * W], in_=out_codes[(e, h)][:].bitcast(I32))
+
+        a_scale_rows = []
+        for pair in range(2):
+            rows_tile = keep.tile([P, INT_PASSES, 2 * W], U8, name="a_scale_rows_%d" % pair, align_bytes=64)
+            nc.vector.memset(rows_tile[:].bitcast(I32), 0)
+            a_scale_rows.append(rows_tile)
+        cond_raw = keep.tile([P, GROUPS, PACK], BF16)
+        emf_raw = keep.tile([P, GROUPS, PACK], BF16)
+        nc.gpsimd.dma_start(out=cond_raw[:], in_=cond.rearrange("(g p t) -> p g t", p=P, t=PACK))
+        nc.gpsimd.dma_start(out=emf_raw[:], in_=emf.rearrange("(g p t) -> p g t", p=P, t=PACK))
+        load_a_words(0, 0)
+        load(("vi", 0, 0))
+        load_a_scales(0)
+        load(("vi", 1, 0))
+        load_a_words(0, 1)
+        load(("vb", 0, 0))
+        load(("d", 0, 0))
+        load(("d", 0, 1))
+        load(("vi", 0, 1))
+        load(("vi", 1, 1))
+        load(("vb", 0, 1))
+        load_a_words(1, 0)
+        load_a_words(1, 1)
+        load_a_scales(1)
+        load(("d", 0, 2))
+        load(("d", 0, 3))
+
+        gain = keep.tile([P, GROUPS * PACK], F32)
+        source_term = keep.tile([P, GROUPS * PACK], F32)
+        out_planes = keep.tile([P, M], U8, align_bytes=64)
+        warm = keep.tile([P, 8], F32)
+        nc.gpsimd.memset(warm[:], 0.0)
+        nc.scalar.activation(out=warm[:], in_=warm[:], func=IDENTITY)
+
+        first = [0, 1, "b"]
+        sort_a_codes(0, 0)
+        sort_a_codes(1, 0)
+        interleave(("vi", 0, 0), "vector", 0, 72)
+        interleave(("vi", 0, 0), "scalar", 72, P)
+        nc.scalar.activation(out=gain[:], in_=cond_raw[:].rearrange("p g t -> p (g t)"), func=IDENTITY)
+        sort_a_scales(0, 0)
+        quantize(("vi", 0, 0))
+        sort_a_scales(1, 0)
+        multiply_pass(0, 0, first, 0)
+        multiply_pass(1, 0, first, 0)
+        interleave(("vi", 1, 0), "scalar")
+        sort_a_scales(0, 1)
+        sort_a_scales(1, 1)
+        sort_a_codes(0, 1)
+        sort_a_codes(1, 1)
+        interleave(("vb", 0, 0), "vector", 0, 96)
+        interleave(("vb", 0, 0), "scalar", 96, P)
+        quantize(("vi", 1, 0))
+        multiply_pass(0, 0, first, 1)
+        multiply_pass(1, 0, first, 1)
+        interleave(("d", 0, 0), "scalar")
+        nc.vector.tensor_tensor(
+            out=source_term[:],
+            in0=cond_raw[:].rearrange("p g t -> p (g t)"),
+            in1=emf_raw[:].rearrange("p g t -> p (g t)"),
+            op=mybir.AluOpType.mult,
+        )
+        quantize(("vb", 0, 0))
+        interleave(("d", 0, 1), "vector")
+        quantize(("d", 0, 0))
+        multiply_pass(0, 0, first, 2)
+        quantize(("d", 0, 1))
+        multiply_pass(1, 0, first, 2)
+        interleave(("vi", 0, 1), "scalar")
+        interleave(("vi", 1, 1), "vector")
+        empty_block(0, 0, 2)
+        quantize(("vi", 0, 1))
+        multiply_pass(0, 1, first, 0)
+        quantize(("vi", 1, 1))
+        multiply_pass(0, 1, first, 1)
+        interleave(("vb", 0, 1), "vector")
+        sort_a_codes(2, 0)
+        quantize(("vb", 0, 1))
+        multiply_pass(0, 1, first, 2)
+        empty_block(1, 0, 2)
+        multiply_block(1, 1)
+        interleave(("d", 0, 2), "vector")
+        sort_a_scales(2, 0)
+        sort_a(2, 1)
+        empty_block(0, 1, 2)
+        quantize(("d", 0, 2))
+        multiply_block(2, 0)
+        interleave(("d", 0, 3), "scalar", 0, SHARE)
+        round_flow(0, 0, "vector")
+        sort_a(3, 0)
+        quantize_flow(0, 0)
+        empty_block(1, 1, 2)
+        store_codes(0, 0)
+        multiply_block(2, 1)
+        round_flow(1, 0, "scalar", 0, SHARE)
+        interleave(("d", 0, 3), "vector", SHARE, P)
+        sort_a(3, 1)
+        round_flow(1, 0, "vector", SHARE, P)
+        quantize(("d", 0, 3))
+        quantize_flow(1, 0)
+        empty_block(2, 0, 2)
+        store_codes(1, 0)
+        multiply_block(3, 0)
+        round_flow(1, 1, "scalar", 0, SHARE)
+        round_flow(0, 1, "vector")
+        round_flow(1, 1, "vector", SHARE, P)
+        quantize_flow(0, 1)
+        empty_block(2, 1, 2)
+        store_codes(0, 1)
+        multiply_block(3, 1)
+        round_flow(2, 1, "scalar", 0, SHARE)
+        round_flow(2, 0, "vector")
+        quantize_flow(1, 1)
+        quantize_flow(2, 0)
+        store_codes(1, 1)
+        store_codes(2, 0)
+        empty_block(3, 0, 2)
+        round_flow(2, 1, "vector", SHARE, P)
+        quantize_flow(2, 1)
+        store_codes(2, 1)
+        round_flow(3, 0, "vector")
+        quantize_flow(3, 0)
+        empty_block(3, 1, 1)
+        store_codes(3, 0)
+        round_flow(3, 1, "scalar", 0, 40)
+        round_flow(3, 1, "vector", 40, P)
+        quantize_flow(3, 1)
+        store_codes(3, 1)
+        for q in range(4):
+            nc.scalar.dma_start(
+                out=out_2.bitcast(I32)[:, 4 * q : 4 * q + 4, :],
+                in_=out_planes[32 * q : 32 * q + 16, :].bitcast(I32),
+            )

@@ -1,6 +1,7 @@
 from contextlib import ExitStack
 
 import concourse.mybir as mybir
+from concourse.masks import make_identity
 
 F32 = mybir.dt.float32
 BF16 = mybir.dt.bfloat16
@@ -58,10 +59,19 @@ def tile_hypergraph_edge_flows_g5_kernel(
             raw[key] = keep.tile([P, PACK, W], BF16, name="raw_%s_%d_%d" % key, align_bytes=64)
             nc.sync.dma_start(out=raw[key][:], in_=source(key))
 
-        def load_a_words(pair, g):
-            raw[("a", pair, g)] = keep.tile([P, 4 * W], U8, name="a_raw_%d_%d" % (pair, g), align_bytes=64)
-            words = a_words.bitcast(I32)[g, :, pair * W : (pair + 1) * W]
-            nc.sync.dma_start(out=raw[("a", pair, g)][:].bitcast(I32), in_=words)
+        def load_a_words(pair, g0, g1):
+            tile = keep.tile([P, g1 - g0, 4 * W], U8, name="a_raw_%d_%d" % (pair, g0), align_bytes=64)
+            words = a_words.bitcast(I32)[g0:g1, :, pair * W : (pair + 1) * W]
+            nc.sync.dma_start(out=tile[:].bitcast(I32), in_=words.rearrange("g p w -> p g w"))
+            for g in range(g0, g1):
+                raw[("a", pair, g)] = tile[:, g - g0, :]
+
+        def load_d_pair(pair):
+            tile = keep.tile([P, PACK, 2 * W], BF16, name="raw_d_pair_%d" % pair, align_bytes=64)
+            rows = d_inc[:, pair * 2 * W : (pair + 1) * 2 * W]
+            nc.sync.dma_start(out=tile[:], in_=rows.rearrange("(p j) w -> p j w", j=PACK))
+            for i in range(2):
+                raw[("d", 0, 2 * pair + i)] = tile[:, :, i * W : (i + 1) * W]
 
         def load_a_scales(pair):
             rows = a_scales.bitcast(I32).rearrange("g (q r) w -> r q g w", r=4)
@@ -148,13 +158,12 @@ def tile_hypergraph_edge_flows_g5_kernel(
         def empty_bank(e, h, t):
             if t == 0:
                 flows[(e, h)] = keep.tile([P, PACK, W], F32, name="flow_%d_%d" % (e, h), align_bytes=64)
-            col = PACK * e + t
             nc.scalar.activation(
                 out=flows[(e, h)][:, t, :],
                 in_=banks[(e, h, t)][:],
                 func=IDENTITY,
-                bias=source_term[:, col : col + 1],
-                scale=gain[:, col : col + 1],
+                bias=source_term[:, t, e : e + 1],
+                scale=gain[:, t, e : e + 1],
             )
 
         def store_flow(e, h, t0, t1):
@@ -189,47 +198,50 @@ def tile_hypergraph_edge_flows_g5_kernel(
             nc.sync.dma_start(out=words[:, h * W : (h + 1) * W], in_=out_codes[(e, h)][:].bitcast(I32))
 
         a_scale_rows = []
+        edge_rows = keep.tile([P, W], BF16, align_bytes=64)
+        nc.vector.memset(edge_rows[:], 0.0)
         for pair in range(2):
             rows_tile = keep.tile([P, INT_PASSES, 2 * W], U8, name="a_scale_rows_%d" % pair, align_bytes=64)
             nc.vector.memset(rows_tile[:].bitcast(I32), 0)
             a_scale_rows.append(rows_tile)
-        cond_raw = keep.tile([P, GROUPS, PACK], BF16)
-        emf_raw = keep.tile([P, GROUPS, PACK], BF16)
-        nc.gpsimd.dma_start(out=cond_raw[:], in_=cond.rearrange("(g p t) -> p g t", p=P, t=PACK))
-        nc.gpsimd.dma_start(out=emf_raw[:], in_=emf.rearrange("(g p t) -> p g t", p=P, t=PACK))
-        load_a_words(0, 0)
+        identity = keep.tile([P, P], BF16, align_bytes=64)
+        make_identity(nc, identity[:])
+        nc.scalar.dma_start(out=edge_rows[0:GROUPS, :], in_=cond.rearrange("(g w) -> g w", w=W))
+        nc.scalar.dma_start(out=edge_rows[GROUPS : 2 * GROUPS, :], in_=emf.rearrange("(g w) -> g w", w=W))
+        load_a_words(0, 0, 1)
         load(("vi", 0, 0))
         load_a_scales(0)
         load(("vi", 1, 0))
-        load_a_words(0, 1)
+        load_a_words(0, 1, 2)
         load(("vb", 0, 0))
         load(("d", 0, 0))
         load(("d", 0, 1))
         load(("vi", 0, 1))
         load(("vi", 1, 1))
         load(("vb", 0, 1))
-        load_a_words(1, 0)
-        load_a_words(1, 1)
+        load_a_words(1, 0, 2)
+        load_d_pair(1)
         load_a_scales(1)
-        load(("d", 0, 2))
-        load(("d", 0, 3))
 
-        gain = keep.tile([P, GROUPS * PACK], F32)
-        source_term = keep.tile([P, GROUPS * PACK], F32)
+        gain = keep.tile([P, PACK, GROUPS], F32)
+        source_term = keep.tile([P, PACK, GROUPS], F32)
         out_planes = keep.tile([P, M], U8, align_bytes=64)
-        warm = keep.tile([P, 8], F32)
-        nc.gpsimd.memset(warm[:], 0.0)
-        nc.scalar.activation(out=warm[:], in_=warm[:], func=IDENTITY)
+        turned = psum.tile([P, PACK, P], BF16, name="bank_7")
+        for t in range(PACK):
+            nc.tensor.transpose(turned[:, t, :], edge_rows[:, t:W:PACK], identity[:])
+        nc.scalar.activation(out=gain[:], in_=turned[:, :, 0:GROUPS], func=IDENTITY)
 
         first = [0, 1, "b"]
         sort_a_codes(0, 0)
         sort_a_codes(1, 0)
         interleave(("vi", 0, 0), "vector", 0, 72)
         interleave(("vi", 0, 0), "scalar", 72, P)
-        nc.scalar.activation(out=gain[:], in_=cond_raw[:].rearrange("p g t -> p (g t)"), func=IDENTITY)
         sort_a_scales(0, 0)
         quantize(("vi", 0, 0))
         sort_a_scales(1, 0)
+        nc.vector.tensor_tensor(
+            out=source_term[:], in0=turned[:, :, GROUPS : 2 * GROUPS], in1=gain[:], op=mybir.AluOpType.mult
+        )
         multiply_pass(0, 0, first, 0)
         multiply_pass(1, 0, first, 0)
         interleave(("vi", 1, 0), "scalar")
@@ -243,12 +255,6 @@ def tile_hypergraph_edge_flows_g5_kernel(
         multiply_pass(0, 0, first, 1)
         multiply_pass(1, 0, first, 1)
         interleave(("d", 0, 0), "scalar")
-        nc.vector.tensor_tensor(
-            out=source_term[:],
-            in0=cond_raw[:].rearrange("p g t -> p (g t)"),
-            in1=emf_raw[:].rearrange("p g t -> p (g t)"),
-            op=mybir.AluOpType.mult,
-        )
         quantize(("vb", 0, 0))
         interleave(("d", 0, 1), "vector")
         quantize(("d", 0, 0))

@@ -21,8 +21,13 @@ W = 512
 GROUPS = E // W
 HALVES = M // W
 INT_PASSES = KI // W
-SHARE = 48
-BLOCKS = [(0, 0), (1, 0), (0, 1), (1, 1), (2, 0), (2, 1), (3, 0), (3, 1)]
+PASSES = [0, 1, "bnd"]
+
+FIRST_SPLIT = 320
+BND_SPLIT = 384
+LAST_D_SPLIT = 192
+ROUND_SPLIT = 208
+TAIL_SPLIT = 320
 
 
 def tile_hypergraph_edge_flows_g5_kernel(
@@ -31,47 +36,36 @@ def tile_hypergraph_edge_flows_g5_kernel(
     nc = tc.nc
     with ExitStack() as ctx:
         keep = ctx.enter_context(tc.tile_pool(name="keep", bufs=1))
-        stage = ctx.enter_context(tc.tile_pool(name="stage", bufs=4))
+        stage = ctx.enter_context(tc.tile_pool(name="stage", bufs=3))
         psum = ctx.enter_context(tc.psum_pool(name="psum", bufs=1))
         ctx.enter_context(tc.manual_schedule())
 
         raw = {}
         grouped = {}
-        quant = {}
-        a_codes = {}
-        a_planes = {}
+        operand = {}
         banks = {}
         flows = {}
         rounded = {}
         out_codes = {}
 
-        def source(key):
-            kind, i, j = key
-            if kind == "vi":
-                rows = v_int[i * W : (i + 1) * W, j * W : (j + 1) * W]
-            elif kind == "vb":
-                rows = v_bnd[:, j * W : (j + 1) * W]
-            else:
-                rows = d_inc[:, j * W : (j + 1) * W]
-            return rows.rearrange("(p j) w -> p j w", j=PACK)
+        def load_rows(keys, rows):
+            tile = keep.tile([P, PACK, len(keys) * W], BF16, name="raw_%s_%s_%s" % keys[0], align_bytes=64)
+            nc.sync.dma_start(out=tile[:], in_=rows.rearrange("(p j) w -> p j w", j=PACK))
+            for i, key in enumerate(keys):
+                raw[key] = tile[:, :, i * W : (i + 1) * W]
 
-        def load(key):
-            raw[key] = keep.tile([P, PACK, W], BF16, name="raw_%s_%d_%d" % key, align_bytes=64)
-            nc.sync.dma_start(out=raw[key][:], in_=source(key))
+        def load_v(which, h):
+            rows = v_bnd if which == "bnd" else v_int[which * W : (which + 1) * W, :]
+            load_rows([("v", which, h)], rows[:, h * W : (h + 1) * W])
+
+        def load_d(e0, e1):
+            load_rows([("a", "bnd", e) for e in range(e0, e1)], d_inc[:, e0 * W : e1 * W])
 
         def load_a_words(pair, g0, g1):
             tile = keep.tile([P, g1 - g0, 4 * W], U8, name="a_raw_%d_%d" % (pair, g0), align_bytes=64)
             words = a_words.bitcast(I32)[g0:g1, :, pair * W : (pair + 1) * W]
             nc.sync.dma_start(out=tile[:].bitcast(I32), in_=words.rearrange("g p w -> p g w"))
-            for g in range(g0, g1):
-                raw[("a", pair, g)] = tile[:, g - g0, :]
-
-        def load_d_pair(pair):
-            tile = keep.tile([P, PACK, 2 * W], BF16, name="raw_d_pair_%d" % pair, align_bytes=64)
-            rows = d_inc[:, pair * 2 * W : (pair + 1) * 2 * W]
-            nc.sync.dma_start(out=tile[:], in_=rows.rearrange("(p j) w -> p j w", j=PACK))
-            for i in range(2):
-                raw[("d", 0, 2 * pair + i)] = tile[:, :, i * W : (i + 1) * W]
+            return tile
 
         def load_a_scales(pair):
             rows = a_scales.bitcast(I32).rearrange("g (q r) w -> r q g w", r=4)
@@ -87,140 +81,153 @@ def tile_hypergraph_edge_flows_g5_kernel(
             else:
                 nc.scalar.copy(out=out, in_=in_)
 
-        def interleave(key, engine, c0=0, c1=P):
-            if key not in grouped:
-                grouped[key] = stage.tile([P, PACK * W], BF16, name="grouped", align_bytes=64)
-            if key[0] == "d":
-                out = grouped[key][:].rearrange("p (t m j) -> p m j t", t=PACK, j=PACK)
-                in_ = raw[key][:].rearrange("p j (m t) -> p m j t", t=PACK)
+        def stage_for(keys):
+            tile = stage.tile([P, len(keys) * PACK * W], BF16, name="grouped", align_bytes=64)
+            grouped[tuple(keys)] = tile
+            for i, key in enumerate(keys):
+                grouped[key] = tile[:, i * PACK * W : (i + 1) * PACK * W]
+
+        def interleave(key, engine, c0=0, c1=W):
+            if key[0] == "a":
+                out = grouped[key].rearrange("p (t c i j) -> p c t i j", t=PACK, i=2, j=PACK)
+                in_ = raw[key].rearrange("p j (c i t) -> p c t i j", t=PACK, i=2)
+                copy_on(engine, out[:, c0 // 8 : c1 // 8], in_[:, c0 // 8 : c1 // 8])
             else:
-                out = grouped[key][:].rearrange("p (c i j) -> p c j i", i=PACK, j=PACK)
-                in_ = raw[key][:].rearrange("p j (c i) -> p c j i", i=PACK)
-            copy_on(engine, out[:, c0:c1], in_[:, c0:c1])
+                out = grouped[key].rearrange("p (c i j) -> p c j i", i=4, j=PACK)
+                in_ = raw[key].rearrange("p j (c i) -> p c j i", i=4)
+                copy_on(engine, out[:, c0 // 4 : c1 // 4], in_[:, c0 // 4 : c1 // 4])
 
-        def quantize(key):
-            codes = keep.tile([P, W], U32, name="codes_%s_%d_%d" % key, align_bytes=64)
-            plane = keep.tile([P, W], U8, name="plane_%s_%d_%d" % key, align_bytes=64)
-            nc.vector.quantize_mx(out=codes[:].bitcast(FP8X4), scales=plane[:], in_=grouped[key][:])
-            quant[key] = (codes, plane)
+        def quantize(keys):
+            codes = keep.tile([P, len(keys) * W], U32, name="codes_%s_%s_%s" % keys[0], align_bytes=64)
+            plane = keep.tile([P, len(keys) * W], U8, name="plane_%s_%s_%s" % keys[0], align_bytes=64)
+            nc.vector.quantize_mx(out=codes[:].bitcast(FP8X4), scales=plane[:], in_=grouped[tuple(keys)][:])
+            for i, key in enumerate(keys):
+                operand[key] = codes[:, i * W : (i + 1) * W].bitcast(FP8X4)
+                operand[key + ("scale",)] = plane[:, i * W : (i + 1) * W]
 
-        def sort_a_codes(e, g):
-            tile = keep.tile([P, PACK, 2 * P], U8, name="a_codes_%d_%d" % (e, g), align_bytes=64)
-            a_codes[(e, g)] = tile
-            words = raw[("a", e // 2, g)][:, e % 2 * 2 * W : (e % 2 + 1) * 2 * W]
+        def sort_a_codes(keys, words):
+            tile = keep.tile([P, 2, 2 * W], U8, name="a_codes_%s_%s_%s" % keys[0], align_bytes=64)
             nc.vector.tensor_copy(
-                out=tile[:].rearrange("p t (m b) -> p t m b", b=2),
-                in_=words.rearrange("p (m t b) -> p t m b", t=PACK, b=2),
+                out=tile[:].rearrange("p n (t m b) -> p n t m b", t=PACK, b=2),
+                in_=words.rearrange("p n (m t b) -> p n t m b", t=PACK, b=2),
             )
+            for i, key in enumerate(keys):
+                operand[key] = tile[:, i, :].bitcast(FP4X4)
 
-        def sort_a_scales(e, g):
-            tile = keep.tile([P, PACK, P], U8, name="a_plane_%d_%d" % (e, g), align_bytes=64)
-            a_planes[(e, g)] = tile
-            rows = a_scale_rows[e // 2][:, g, e % 2 * W : (e % 2 + 1) * W]
-            nc.vector.tensor_copy(out=tile[:], in_=rows.rearrange("p (m t) -> p t m", t=PACK))
+        def sort_a_scales(keys, rows):
+            tile = keep.tile([P, 2, W], U8, name="a_plane_%s_%s_%s" % keys[0], align_bytes=64)
+            nc.vector.tensor_copy(
+                out=tile[:].rearrange("p n (t m) -> p n t m", t=PACK),
+                in_=rows.rearrange("p n (m t) -> p n t m", t=PACK),
+            )
+            for i, key in enumerate(keys):
+                operand[key + ("scale",)] = tile[:, i, :]
 
-        def sort_a(e, g):
-            sort_a_codes(e, g)
-            sort_a_scales(e, g)
+        def open_bank(key, bank):
+            banks[key] = psum.tile([P, W], F32, name="bank_%d" % bank)
 
-        def multiply(e, h, t, which, start, stop):
-            if start:
-                bank = BLOCKS.index((e, h)) % 2 * PACK + t
-                banks[(e, h, t)] = psum.tile([P, W], F32, name="bank_%d" % bank)
-            if which == "b":
-                codes, plane = quant[("d", 0, e)]
-                lhs = codes[:, t * P : (t + 1) * P].bitcast(FP8X4)
-                lhs_scale = plane[:, t * P : (t + 1) * P]
-                codes, plane = quant[("vb", 0, h)]
-            else:
-                lhs = a_codes[(e, which)][:, t, :].bitcast(FP4X4)
-                lhs_scale = a_planes[(e, which)][:, t, :]
-                codes, plane = quant[("vi", which, h)]
+        def multiply(key, which, c0=0, c1=W):
+            e, h, t = key[0:3]
             nc.tensor.matmul_mx(
-                out=banks[(e, h, t)][:],
-                lhsT=lhs,
-                lhsT_scale=lhs_scale,
-                rhs=codes[:].bitcast(FP8X4),
-                rhs_scale=plane[:],
-                start=start,
-                stop=stop,
+                out=banks[key][:, c0:c1],
+                lhsT=operand[("a", which, e)][:, t * P : (t + 1) * P],
+                lhsT_scale=operand[("a", which, e, "scale")][:, t * P : (t + 1) * P],
+                rhs=operand[("v", which, h)][:, c0:c1],
+                rhs_scale=operand[("v", which, h, "scale")][:, c0:c1],
+                start=which == PASSES[0],
+                stop=which == PASSES[-1],
             )
 
-        def multiply_pass(e, h, order, n):
+        def multiply_pass(e, h, which):
             for t in range(PACK):
-                multiply(e, h, t, order[n], n == 0, n == len(order) - 1)
+                if which == PASSES[0]:
+                    open_bank((e, h, t), e * PACK + t)
+                multiply((e, h, t), which)
+
+        def multiply_bank(e, h, t):
+            open_bank((e, h, t), (e if e < 2 else h) * PACK + t)
+            for which in PASSES:
+                multiply((e, h, t), which)
 
         def multiply_block(e, h):
             for t in range(PACK):
-                for n, which in enumerate([0, 1, "b"]):
-                    multiply(e, h, t, which, n == 0, n == 2)
+                multiply_bank(e, h, t)
 
-        def empty_bank(e, h, t):
-            if t == 0:
-                flows[(e, h)] = keep.tile([P, PACK, W], F32, name="flow_%d_%d" % (e, h), align_bytes=64)
+        def multiply_narrow(e, h, t, part, bank):
+            open_bank((e, h, t, part), bank)
+            for c0 in range(part * W // 2, (part + 1) * W // 2, P):
+                for which in PASSES:
+                    multiply((e, h, t, part), which, c0, c0 + P)
+
+        def empty_bank(key, c0=0, c1=W):
+            e, h, t = key[0:3]
+            if e not in flows:
+                flows[e] = keep.tile([P, PACK, M], F32, name="flow_%d" % e, align_bytes=64)
             nc.scalar.activation(
-                out=flows[(e, h)][:, t, :],
-                in_=banks[(e, h, t)][:],
+                out=flows[e][:, t, h * W + c0 : h * W + c1],
+                in_=banks[key][:, c0:c1],
                 func=IDENTITY,
                 bias=source_term[:, t, e : e + 1],
                 scale=gain[:, t, e : e + 1],
             )
 
-        def store_flow(e, h, t0, t1):
-            rows = out_0[e * W : (e + 1) * W, h * W : (h + 1) * W].rearrange("(p t) m -> p t m", t=PACK)
-            nc.sync.dma_start(out=rows[:, t0:t1, :], in_=flows[(e, h)][:, t0:t1, :])
+        def store_flow(e, t0, t1, m0, m1):
+            rows = out_0[e * W : (e + 1) * W, :].rearrange("(p t) m -> p t m", t=PACK)
+            nc.sync.dma_start(out=rows[:, t0:t1, m0:m1], in_=flows[e][:, t0:t1, m0:m1])
 
         def empty_block(e, h, step):
             for t in range(PACK):
-                empty_bank(e, h, t)
+                empty_bank((e, h, t))
                 if (t + 1) % step == 0:
-                    store_flow(e, h, t + 1 - step, t + 1)
+                    store_flow(e, t + 1 - step, t + 1, h * W, (h + 1) * W)
 
-        def round_flow(e, h, engine, c0=0, c1=P):
-            if (e, h) not in rounded:
-                rounded[(e, h)] = stage.tile([P, PACK * W], BF16, name="rounded", align_bytes=64)
+        def round_flow(e, engine, m0, m1):
+            if e not in rounded:
+                rounded[e] = stage.tile([P, PACK * M], BF16, name="rounded", bufs=2, align_bytes=64)
             copy_on(
                 engine,
-                rounded[(e, h)][:].rearrange("p (c i t) -> p c t i", i=PACK, t=PACK)[:, c0:c1],
-                flows[(e, h)][:].rearrange("p t (c i) -> p c t i", i=PACK)[:, c0:c1],
+                rounded[e][:].rearrange("p (c i t) -> p c t i", i=4, t=PACK)[:, m0 // 4 : m1 // 4],
+                flows[e][:].rearrange("p t (c i) -> p c t i", i=4)[:, m0 // 4 : m1 // 4],
             )
 
-        def quantize_flow(e, h):
-            out_codes[(e, h)] = keep.tile([P, W], U32, name="out_codes_%d_%d" % (e, h), align_bytes=64)
+        def quantize_flow(e, m0, m1):
+            if e not in out_codes:
+                out_codes[e] = keep.tile([P, M], U32, name="out_codes_%d" % e, align_bytes=64)
             nc.vector.quantize_mx(
-                out=out_codes[(e, h)][:].bitcast(FP8X4),
-                scales=out_planes[PACK * e : P, h * W : (h + 1) * W],
-                in_=rounded[(e, h)][:],
+                out=out_codes[e][:, m0:m1].bitcast(FP8X4),
+                scales=out_planes[PACK * e : P, m0:m1],
+                in_=rounded[e][:, PACK * m0 : PACK * m1],
             )
 
-        def store_codes(e, h):
+        def store_codes(e, m0, m1):
             words = out_1[e].rearrange("p m t -> p (m t)").bitcast(I32)
-            nc.sync.dma_start(out=words[:, h * W : (h + 1) * W], in_=out_codes[(e, h)][:].bitcast(I32))
+            nc.sync.dma_start(out=words[:, m0:m1], in_=out_codes[e][:, m0:m1].bitcast(I32))
 
-        a_scale_rows = []
         edge_rows = keep.tile([P, W], BF16, align_bytes=64)
         nc.vector.memset(edge_rows[:], 0.0)
+        a_scale_rows = []
         for pair in range(2):
             rows_tile = keep.tile([P, INT_PASSES, 2 * W], U8, name="a_scale_rows_%d" % pair, align_bytes=64)
             nc.vector.memset(rows_tile[:].bitcast(I32), 0)
             a_scale_rows.append(rows_tile)
-        identity = keep.tile([P, P], BF16, align_bytes=64)
-        make_identity(nc, identity[:])
+        identity_f32 = keep.tile([P, P], F32, align_bytes=64)
+        make_identity(nc, identity_f32[:])
         nc.scalar.dma_start(out=edge_rows[0:GROUPS, :], in_=cond.rearrange("(g w) -> g w", w=W))
         nc.scalar.dma_start(out=edge_rows[GROUPS : 2 * GROUPS, :], in_=emf.rearrange("(g w) -> g w", w=W))
-        load_a_words(0, 0, 1)
-        load(("vi", 0, 0))
+        identity = keep.tile([P, P], BF16, align_bytes=64)
+        nc.scalar.activation(out=identity[:], in_=identity_f32[:], func=IDENTITY)
+        early_words = [load_a_words(0, 0, 1)]
+        load_v(0, 0)
         load_a_scales(0)
-        load(("vi", 1, 0))
-        load_a_words(0, 1, 2)
-        load(("vb", 0, 0))
-        load(("d", 0, 0))
-        load(("d", 0, 1))
-        load(("vi", 0, 1))
-        load(("vi", 1, 1))
-        load(("vb", 0, 1))
-        load_a_words(1, 0, 2)
-        load_d_pair(1)
+        load_v(1, 0)
+        early_words.append(load_a_words(0, 1, 2))
+        load_v("bnd", 0)
+        load_d(0, 1)
+        load_d(1, 2)
+        for which in PASSES:
+            load_v(which, 1)
+        late_words = load_a_words(1, 0, 2)
+        load_d(2, 4)
         load_a_scales(1)
 
         gain = keep.tile([P, PACK, GROUPS], F32)
@@ -229,98 +236,117 @@ def tile_hypergraph_edge_flows_g5_kernel(
         turned = psum.tile([P, PACK, P], BF16, name="bank_7")
         for t in range(PACK):
             nc.tensor.transpose(turned[:, t, :], edge_rows[:, t:W:PACK], identity[:])
-        nc.scalar.activation(out=gain[:], in_=turned[:, :, 0:GROUPS], func=IDENTITY)
 
-        first = [0, 1, "b"]
-        sort_a_codes(0, 0)
-        sort_a_codes(1, 0)
-        interleave(("vi", 0, 0), "vector", 0, 72)
-        interleave(("vi", 0, 0), "scalar", 72, P)
-        sort_a_scales(0, 0)
-        quantize(("vi", 0, 0))
-        sort_a_scales(1, 0)
+        def early_codes(g):
+            sort_a_codes([("a", g, 0), ("a", g, 1)], early_words[g][:, 0, :].rearrange("p (n w) -> p n w", n=2))
+
+        def early_scales(g):
+            sort_a_scales([("a", g, 0), ("a", g, 1)], a_scale_rows[0][:, g, :].rearrange("p (n w) -> p n w", n=2))
+
+        def late_codes(e):
+            sort_a_codes([("a", 0, e), ("a", 1, e)], late_words[:, :, (e - 2) * 2 * W : (e - 1) * 2 * W])
+
+        def late_scales(e):
+            sort_a_scales([("a", 0, e), ("a", 1, e)], a_scale_rows[1][:, :, (e - 2) * W : (e - 1) * W])
+
+        v00, v10, vb0 = ("v", 0, 0), ("v", 1, 0), ("v", "bnd", 0)
+        v01, v11, vb1 = ("v", 0, 1), ("v", 1, 1), ("v", "bnd", 1)
+        d0, d1, d2, d3 = [("a", "bnd", e) for e in range(GROUPS)]
+
+        early_codes(0)
+        stage_for([v00])
+        interleave(v00, "vector", 0, FIRST_SPLIT)
+        interleave(v00, "scalar", FIRST_SPLIT, W)
+        nc.scalar.copy(out=gain[:], in_=turned[:, :, 0:GROUPS])
+        early_scales(0)
+        quantize([v00])
+        multiply_pass(0, 0, 0)
         nc.vector.tensor_tensor(
             out=source_term[:], in0=turned[:, :, GROUPS : 2 * GROUPS], in1=gain[:], op=mybir.AluOpType.mult
         )
-        multiply_pass(0, 0, first, 0)
-        multiply_pass(1, 0, first, 0)
-        interleave(("vi", 1, 0), "scalar")
-        sort_a_scales(0, 1)
-        sort_a_scales(1, 1)
-        sort_a_codes(0, 1)
-        sort_a_codes(1, 1)
-        interleave(("vb", 0, 0), "vector", 0, 96)
-        interleave(("vb", 0, 0), "scalar", 96, P)
-        quantize(("vi", 1, 0))
-        multiply_pass(0, 0, first, 1)
-        multiply_pass(1, 0, first, 1)
-        interleave(("d", 0, 0), "scalar")
-        quantize(("vb", 0, 0))
-        interleave(("d", 0, 1), "vector")
-        quantize(("d", 0, 0))
-        multiply_pass(0, 0, first, 2)
-        quantize(("d", 0, 1))
-        multiply_pass(1, 0, first, 2)
-        interleave(("vi", 0, 1), "scalar")
-        interleave(("vi", 1, 1), "vector")
+        multiply_pass(1, 0, 0)
+        stage_for([v10, vb0])
+        interleave(v10, "scalar")
+        early_codes(1)
+        interleave(vb0, "vector", 0, BND_SPLIT)
+        interleave(vb0, "scalar", BND_SPLIT, W)
+        early_scales(1)
+        quantize([v10, vb0])
+        multiply_pass(0, 0, 1)
+        multiply_pass(1, 0, 1)
+        stage_for([d0, d1])
+        interleave(d0, "scalar")
+        interleave(d1, "vector")
+        stage_for([v01, v11])
+        interleave(v01, "scalar")
+        quantize([d0, d1])
+        multiply_pass(0, 0, "bnd")
+        multiply_pass(1, 0, "bnd")
+        interleave(v11, "vector")
         empty_block(0, 0, 2)
-        quantize(("vi", 0, 1))
-        multiply_pass(0, 1, first, 0)
-        quantize(("vi", 1, 1))
-        multiply_pass(0, 1, first, 1)
-        interleave(("vb", 0, 1), "vector")
-        sort_a_codes(2, 0)
-        quantize(("vb", 0, 1))
-        multiply_pass(0, 1, first, 2)
+        stage_for([vb1])
+        quantize([v01, v11])
+        multiply_pass(0, 1, 0)
+        multiply_pass(0, 1, 1)
+        interleave(vb1, "vector")
+        quantize([vb1])
+        multiply_pass(0, 1, "bnd")
         empty_block(1, 0, 2)
         multiply_block(1, 1)
-        interleave(("d", 0, 2), "vector")
-        sort_a_scales(2, 0)
-        sort_a(2, 1)
+        late_codes(2)
+        stage_for([d2])
+        interleave(d2, "vector")
+        late_scales(2)
         empty_block(0, 1, 2)
-        quantize(("d", 0, 2))
+        quantize([d2])
         multiply_block(2, 0)
-        interleave(("d", 0, 3), "scalar", 0, SHARE)
-        round_flow(0, 0, "vector")
-        sort_a(3, 0)
-        quantize_flow(0, 0)
+        round_flow(0, "vector", 0, W)
+        round_flow(0, "vector", W, M)
+        quantize_flow(0, 0, M)
         empty_block(1, 1, 2)
-        store_codes(0, 0)
         multiply_block(2, 1)
-        round_flow(1, 0, "scalar", 0, SHARE)
-        interleave(("d", 0, 3), "vector", SHARE, P)
-        sort_a(3, 1)
-        round_flow(1, 0, "vector", SHARE, P)
-        quantize(("d", 0, 3))
-        quantize_flow(1, 0)
+        stage_for([d3])
+        interleave(d3, "scalar", 0, LAST_D_SPLIT)
+        late_codes(3)
+        interleave(d3, "vector", LAST_D_SPLIT, W)
+        late_scales(3)
+        quantize([d3])
         empty_block(2, 0, 2)
-        store_codes(1, 0)
+        store_codes(0, 0, M)
         multiply_block(3, 0)
-        round_flow(1, 1, "scalar", 0, SHARE)
-        round_flow(0, 1, "vector")
-        round_flow(1, 1, "vector", SHARE, P)
-        quantize_flow(0, 1)
+        round_flow(1, "scalar", M - ROUND_SPLIT, M)
+        round_flow(1, "vector", 0, W)
+        round_flow(1, "vector", W, M - ROUND_SPLIT)
+        quantize_flow(1, 0, W)
+        quantize_flow(1, W, M)
         empty_block(2, 1, 2)
-        store_codes(0, 1)
-        multiply_block(3, 1)
-        round_flow(2, 1, "scalar", 0, SHARE)
-        round_flow(2, 0, "vector")
-        quantize_flow(1, 1)
-        quantize_flow(2, 0)
-        store_codes(1, 1)
-        store_codes(2, 0)
+        store_codes(1, 0, M)
+        for t in range(PACK - 1):
+            multiply_bank(3, 1, t)
+        multiply_narrow(3, 1, 3, 0, 7)
+        round_flow(2, "scalar", M - ROUND_SPLIT, M)
+        round_flow(2, "vector", 0, W)
+        round_flow(2, "vector", W, M - ROUND_SPLIT)
+        quantize_flow(2, 0, W)
+        quantize_flow(2, W, M)
         empty_block(3, 0, 2)
-        round_flow(2, 1, "vector", SHARE, P)
-        quantize_flow(2, 1)
-        store_codes(2, 1)
-        round_flow(3, 0, "vector")
-        quantize_flow(3, 0)
-        empty_block(3, 1, 1)
-        store_codes(3, 0)
-        round_flow(3, 1, "scalar", 0, 40)
-        round_flow(3, 1, "vector", 40, P)
-        quantize_flow(3, 1)
-        store_codes(3, 1)
+        multiply_narrow(3, 1, 3, 1, 0)
+        store_codes(2, 0, M)
+        round_flow(3, "vector", 0, W)
+        empty_bank((3, 1, 0))
+        empty_bank((3, 1, 1))
+        store_flow(3, 0, 2, W, M)
+        empty_bank((3, 1, 2))
+        empty_bank((3, 1, 3, 0), 0, W // 2)
+        empty_bank((3, 1, 3, 1), W // 2, W)
+        store_flow(3, 2, 4, W, M)
+        round_flow(3, "scalar", M - TAIL_SPLIT, M)
+        round_flow(3, "vector", W, M - TAIL_SPLIT)
+        quantize_flow(3, 0, W)
+        store_codes(3, 0, W)
+        quantize_flow(3, W, M)
+        store_codes(3, W, M)
+
         for q in range(4):
             nc.scalar.dma_start(
                 out=out_2.bitcast(I32)[:, 4 * q : 4 * q + 4, :],

@@ -23,11 +23,11 @@ HALVES = M // W
 INT_PASSES = KI // W
 PASSES = [0, 1, "bnd"]
 
-FIRST_SPLIT = 320
-BND_SPLIT = 384
+FIRST_SPLIT = 128
+BND_SPLIT = 256
 LAST_D_SPLIT = 192
-ROUND_SPLIT = 208
-TAIL_SPLIT = 320
+ROUND_SPLIT = 192
+TAIL_SPLIT = 256
 
 
 def tile_hypergraph_edge_flows_g5_kernel(
@@ -36,7 +36,7 @@ def tile_hypergraph_edge_flows_g5_kernel(
     nc = tc.nc
     with ExitStack() as ctx:
         keep = ctx.enter_context(tc.tile_pool(name="keep", bufs=1))
-        stage = ctx.enter_context(tc.tile_pool(name="stage", bufs=3))
+        stage = ctx.enter_context(tc.tile_pool(name="stage", bufs=5))
         psum = ctx.enter_context(tc.psum_pool(name="psum", bufs=1))
         ctx.enter_context(tc.manual_schedule())
 
@@ -126,23 +126,23 @@ def tile_hypergraph_edge_flows_g5_kernel(
         def open_bank(key, bank):
             banks[key] = psum.tile([P, W], F32, name="bank_%d" % bank)
 
-        def multiply(key, which, c0=0, c1=W):
-            e, h, t = key[0:3]
+        def multiply(key, which, order=PASSES):
+            e, h, t = key
             nc.tensor.matmul_mx(
-                out=banks[key][:, c0:c1],
+                out=banks[key][:],
                 lhsT=operand[("a", which, e)][:, t * P : (t + 1) * P],
                 lhsT_scale=operand[("a", which, e, "scale")][:, t * P : (t + 1) * P],
-                rhs=operand[("v", which, h)][:, c0:c1],
-                rhs_scale=operand[("v", which, h, "scale")][:, c0:c1],
-                start=which == PASSES[0],
-                stop=which == PASSES[-1],
+                rhs=operand[("v", which, h)],
+                rhs_scale=operand[("v", which, h, "scale")],
+                start=which == order[0],
+                stop=which == order[-1],
             )
 
-        def multiply_pass(e, h, which):
+        def multiply_pass(e, h, which, order=PASSES):
             for t in range(PACK):
-                if which == PASSES[0]:
+                if which == order[0]:
                     open_bank((e, h, t), e * PACK + t)
-                multiply((e, h, t), which)
+                multiply((e, h, t), which, order)
 
         def multiply_bank(e, h, t):
             open_bank((e, h, t), (e if e < 2 else h) * PACK + t)
@@ -153,41 +153,38 @@ def tile_hypergraph_edge_flows_g5_kernel(
             for t in range(PACK):
                 multiply_bank(e, h, t)
 
-        def multiply_narrow(e, h, t, part, bank):
-            open_bank((e, h, t, part), bank)
-            for c0 in range(part * W // 2, (part + 1) * W // 2, P):
-                for which in PASSES:
-                    multiply((e, h, t, part), which, c0, c0 + P)
-
-        def empty_bank(key, c0=0, c1=W):
-            e, h, t = key[0:3]
-            if e not in flows:
-                flows[e] = keep.tile([P, PACK, M], F32, name="flow_%d" % e, align_bytes=64)
+        def empty_bank(e, h, t):
+            if t == 0:
+                flows[(e, h)] = keep.tile([P, PACK, W], F32, name="flow_%d_%d" % (e, h), align_bytes=64)
             nc.scalar.activation(
-                out=flows[e][:, t, h * W + c0 : h * W + c1],
-                in_=banks[key][:, c0:c1],
+                out=flows[(e, h)][:, t, :],
+                in_=banks[(e, h, t)][:],
                 func=IDENTITY,
                 bias=source_term[:, t, e : e + 1],
                 scale=gain[:, t, e : e + 1],
             )
 
-        def store_flow(e, t0, t1, m0, m1):
-            rows = out_0[e * W : (e + 1) * W, :].rearrange("(p t) m -> p t m", t=PACK)
-            nc.sync.dma_start(out=rows[:, t0:t1, m0:m1], in_=flows[e][:, t0:t1, m0:m1])
+        def store_flow(e, h, t0, t1):
+            rows = out_0[e * W : (e + 1) * W, h * W : (h + 1) * W].rearrange("(p t) m -> p t m", t=PACK)
+            nc.sync.dma_start(out=rows[:, t0:t1, :], in_=flows[(e, h)][:, t0:t1, :])
 
-        def empty_block(e, h, step):
+        def empty_block(e, h, step, between=()):
             for t in range(PACK):
-                empty_bank((e, h, t))
+                empty_bank(e, h, t)
                 if (t + 1) % step == 0:
-                    store_flow(e, t + 1 - step, t + 1, h * W, (h + 1) * W)
+                    store_flow(e, h, t + 1 - step, t + 1)
+                if t == 1:
+                    for args in between:
+                        store_codes(*args)
 
-        def round_flow(e, engine, m0, m1):
+        def round_flow(e, h, engine, c0=0, c1=W):
             if e not in rounded:
                 rounded[e] = stage.tile([P, PACK * M], BF16, name="rounded", bufs=2, align_bytes=64)
+            half = rounded[e][:, h * PACK * W : (h + 1) * PACK * W]
             copy_on(
                 engine,
-                rounded[e][:].rearrange("p (c i t) -> p c t i", i=4, t=PACK)[:, m0 // 4 : m1 // 4],
-                flows[e][:].rearrange("p t (c i) -> p c t i", i=4)[:, m0 // 4 : m1 // 4],
+                half.rearrange("p (c i t) -> p c t i", i=4, t=PACK)[:, c0 // 4 : c1 // 4],
+                flows[(e, h)][:].rearrange("p t (c i) -> p c t i", i=4)[:, c0 // 4 : c1 // 4],
             )
 
         def quantize_flow(e, m0, m1):
@@ -212,12 +209,12 @@ def tile_hypergraph_edge_flows_g5_kernel(
             a_scale_rows.append(rows_tile)
         identity_f32 = keep.tile([P, P], F32, align_bytes=64)
         make_identity(nc, identity_f32[:])
+        early_words = [load_a_words(0, 0, 1)]
+        load_v(0, 0)
         nc.scalar.dma_start(out=edge_rows[0:GROUPS, :], in_=cond.rearrange("(g w) -> g w", w=W))
         nc.scalar.dma_start(out=edge_rows[GROUPS : 2 * GROUPS, :], in_=emf.rearrange("(g w) -> g w", w=W))
         identity = keep.tile([P, P], BF16, align_bytes=64)
         nc.scalar.activation(out=identity[:], in_=identity_f32[:], func=IDENTITY)
-        early_words = [load_a_words(0, 0, 1)]
-        load_v(0, 0)
         load_a_scales(0)
         load_v(1, 0)
         early_words.append(load_a_words(0, 1, 2))
@@ -259,38 +256,45 @@ def tile_hypergraph_edge_flows_g5_kernel(
         interleave(v00, "scalar", FIRST_SPLIT, W)
         nc.scalar.copy(out=gain[:], in_=turned[:, :, 0:GROUPS])
         early_scales(0)
+        early_scales(1)
         quantize([v00])
         multiply_pass(0, 0, 0)
         nc.vector.tensor_tensor(
             out=source_term[:], in0=turned[:, :, GROUPS : 2 * GROUPS], in1=gain[:], op=mybir.AluOpType.mult
         )
         multiply_pass(1, 0, 0)
-        stage_for([v10, vb0])
+        stage_for([v10])
         interleave(v10, "scalar")
         early_codes(1)
+        stage_for([vb0])
         interleave(vb0, "vector", 0, BND_SPLIT)
         interleave(vb0, "scalar", BND_SPLIT, W)
-        early_scales(1)
-        quantize([v10, vb0])
+        quantize([v10])
         multiply_pass(0, 0, 1)
         multiply_pass(1, 0, 1)
-        stage_for([d0, d1])
-        interleave(d0, "scalar")
-        interleave(d1, "vector")
-        stage_for([v01, v11])
-        interleave(v01, "scalar")
-        quantize([d0, d1])
+        stage_for([d0])
+        interleave(d0, "vector")
+        stage_for([d1])
+        interleave(d1, "scalar")
+        quantize([vb0])
+        quantize([d0])
         multiply_pass(0, 0, "bnd")
-        multiply_pass(1, 0, "bnd")
+        stage_for([v01])
+        interleave(v01, "scalar", 128, W)
+        stage_for([v11])
         interleave(v11, "vector")
-        empty_block(0, 0, 2)
+        quantize([d1])
+        multiply_pass(1, 0, "bnd")
+        quantize([v11])
         stage_for([vb1])
-        quantize([v01, v11])
-        multiply_pass(0, 1, 0)
-        multiply_pass(0, 1, 1)
         interleave(vb1, "vector")
+        interleave(v01, "vector", 0, 128)
+        empty_block(0, 0, 2)
+        multiply_pass(0, 1, 1, [1, "bnd", 0])
         quantize([vb1])
-        multiply_pass(0, 1, "bnd")
+        multiply_pass(0, 1, "bnd", [1, "bnd", 0])
+        quantize([v01])
+        multiply_pass(0, 1, 0, [1, "bnd", 0])
         empty_block(1, 0, 2)
         multiply_block(1, 1)
         late_codes(2)
@@ -300,10 +304,12 @@ def tile_hypergraph_edge_flows_g5_kernel(
         empty_block(0, 1, 2)
         quantize([d2])
         multiply_block(2, 0)
-        round_flow(0, "vector", 0, W)
-        round_flow(0, "vector", W, M)
-        quantize_flow(0, 0, M)
+        round_flow(0, 0, "vector")
+        round_flow(0, 1, "vector")
+        quantize_flow(0, 0, W)
+        quantize_flow(0, W, M)
         empty_block(1, 1, 2)
+        store_codes(0, 0, W)
         multiply_block(2, 1)
         stage_for([d3])
         interleave(d3, "scalar", 0, LAST_D_SPLIT)
@@ -311,37 +317,28 @@ def tile_hypergraph_edge_flows_g5_kernel(
         interleave(d3, "vector", LAST_D_SPLIT, W)
         late_scales(3)
         quantize([d3])
-        empty_block(2, 0, 2)
-        store_codes(0, 0, M)
+        empty_block(2, 0, 2, [(0, W, M)])
         multiply_block(3, 0)
-        round_flow(1, "scalar", M - ROUND_SPLIT, M)
-        round_flow(1, "vector", 0, W)
-        round_flow(1, "vector", W, M - ROUND_SPLIT)
+        round_flow(1, 1, "scalar", W - ROUND_SPLIT, W)
+        round_flow(1, 0, "vector")
+        round_flow(1, 1, "vector", 0, W - ROUND_SPLIT)
         quantize_flow(1, 0, W)
         quantize_flow(1, W, M)
         empty_block(2, 1, 2)
-        store_codes(1, 0, M)
-        for t in range(PACK - 1):
-            multiply_bank(3, 1, t)
-        multiply_narrow(3, 1, 3, 0, 7)
-        round_flow(2, "scalar", M - ROUND_SPLIT, M)
-        round_flow(2, "vector", 0, W)
-        round_flow(2, "vector", W, M - ROUND_SPLIT)
+        store_codes(1, 0, W)
+        store_codes(1, W, M)
+        multiply_block(3, 1)
+        round_flow(2, 1, "scalar", W - ROUND_SPLIT, W)
+        round_flow(2, 0, "vector")
+        round_flow(2, 1, "vector", 0, W - ROUND_SPLIT)
         quantize_flow(2, 0, W)
         quantize_flow(2, W, M)
         empty_block(3, 0, 2)
-        multiply_narrow(3, 1, 3, 1, 0)
-        store_codes(2, 0, M)
-        round_flow(3, "vector", 0, W)
-        empty_bank((3, 1, 0))
-        empty_bank((3, 1, 1))
-        store_flow(3, 0, 2, W, M)
-        empty_bank((3, 1, 2))
-        empty_bank((3, 1, 3, 0), 0, W // 2)
-        empty_bank((3, 1, 3, 1), W // 2, W)
-        store_flow(3, 2, 4, W, M)
-        round_flow(3, "scalar", M - TAIL_SPLIT, M)
-        round_flow(3, "vector", W, M - TAIL_SPLIT)
+        store_codes(2, 0, W)
+        round_flow(3, 0, "vector")
+        empty_block(3, 1, 2, [(2, W, M)])
+        round_flow(3, 1, "scalar", W - TAIL_SPLIT, W)
+        round_flow(3, 1, "vector", 0, W - TAIL_SPLIT)
         quantize_flow(3, 0, W)
         store_codes(3, 0, W)
         quantize_flow(3, W, M)

from contextlib import ExitStack

import concourse.mybir as mybir
from concourse.masks import make_identity

F32 = mybir.dt.float32
BF16 = mybir.dt.bfloat16
I32 = mybir.dt.int32
U32 = mybir.dt.uint32
U8 = mybir.dt.uint8
FP8X4 = mybir.dt.float8_e4m3fn_x4
FP4X4 = mybir.dt.float4_e2m1fn_x4
IDENTITY = mybir.ActivationFunctionType.Identity

M, E, KI, KB = 1024, 2048, 1024, 512
FLOPS = 2 * E * M * (KI + KB)

P = 128
PACK = 4
W = 512
GROUPS = E // W
HALVES = M // W
INT_PASSES = KI // W
PASSES = [0, 1, "bnd"]

FIRST_SPLIT = 128
BND_SPLIT = 256
LAST_D_SPLIT = 192
ROUND_SPLIT = 192
TAIL_SPLIT = 256


def tile_hypergraph_edge_flows_g5_kernel(
    tc, a_words, a_scales, v_int, d_inc, v_bnd, emf, cond, out_0, out_1, out_2
):
    nc = tc.nc
    with ExitStack() as ctx:
        keep = ctx.enter_context(tc.tile_pool(name="keep", bufs=1))
        stage = ctx.enter_context(tc.tile_pool(name="stage", bufs=5))
        psum = ctx.enter_context(tc.psum_pool(name="psum", bufs=1))
        ctx.enter_context(tc.manual_schedule())

        raw = {}
        grouped = {}
        operand = {}
        banks = {}
        flows = {}
        rounded = {}
        out_codes = {}

        def load_rows(keys, rows):
            tile = keep.tile([P, PACK, len(keys) * W], BF16, name="raw_%s_%s_%s" % keys[0], align_bytes=64)
            nc.sync.dma_start(out=tile[:], in_=rows.rearrange("(p j) w -> p j w", j=PACK))
            for i, key in enumerate(keys):
                raw[key] = tile[:, :, i * W : (i + 1) * W]

        def load_v(which, h):
            rows = v_bnd if which == "bnd" else v_int[which * W : (which + 1) * W, :]
            load_rows([("v", which, h)], rows[:, h * W : (h + 1) * W])

        def load_d(e0, e1):
            load_rows([("a", "bnd", e) for e in range(e0, e1)], d_inc[:, e0 * W : e1 * W])

        def load_a_words(pair, g0, g1):
            tile = keep.tile([P, g1 - g0, 4 * W], U8, name="a_raw_%d_%d" % (pair, g0), align_bytes=64)
            words = a_words.bitcast(I32)[g0:g1, :, pair * W : (pair + 1) * W]
            nc.sync.dma_start(out=tile[:].bitcast(I32), in_=words.rearrange("g p w -> p g w"))
            return tile

        def load_a_scales(pair):
            rows = a_scales.bitcast(I32).rearrange("g (q r) w -> r q g w", r=4)
            for r in range(4):
                nc.sync.dma_start(
                    out=a_scale_rows[pair][r:P:32, :, :].bitcast(I32),
                    in_=rows[r, :, :, pair * W // 2 : (pair + 1) * W // 2],
                )

        def copy_on(engine, out, in_):
            if engine == "vector":
                nc.vector.tensor_copy(out=out, in_=in_)
            else:
                nc.scalar.copy(out=out, in_=in_)

        def stage_for(keys):
            tile = stage.tile([P, len(keys) * PACK * W], BF16, name="grouped", align_bytes=64)
            grouped[tuple(keys)] = tile
            for i, key in enumerate(keys):
                grouped[key] = tile[:, i * PACK * W : (i + 1) * PACK * W]

        def interleave(key, engine, c0=0, c1=W):
            if key[0] == "a":
                out = grouped[key].rearrange("p (t c i j) -> p c t i j", t=PACK, i=2, j=PACK)
                in_ = raw[key].rearrange("p j (c i t) -> p c t i j", t=PACK, i=2)
                copy_on(engine, out[:, c0 // 8 : c1 // 8], in_[:, c0 // 8 : c1 // 8])
            else:
                out = grouped[key].rearrange("p (c i j) -> p c j i", i=4, j=PACK)
                in_ = raw[key].rearrange("p j (c i) -> p c j i", i=4)
                copy_on(engine, out[:, c0 // 4 : c1 // 4], in_[:, c0 // 4 : c1 // 4])

        def quantize(keys):
            codes = keep.tile([P, len(keys) * W], U32, name="codes_%s_%s_%s" % keys[0], align_bytes=64)
            plane = keep.tile([P, len(keys) * W], U8, name="plane_%s_%s_%s" % keys[0], align_bytes=64)
            nc.vector.quantize_mx(out=codes[:].bitcast(FP8X4), scales=plane[:], in_=grouped[tuple(keys)][:])
            for i, key in enumerate(keys):
                operand[key] = codes[:, i * W : (i + 1) * W].bitcast(FP8X4)
                operand[key + ("scale",)] = plane[:, i * W : (i + 1) * W]

        def sort_a_codes(keys, words):
            tile = keep.tile([P, 2, 2 * W], U8, name="a_codes_%s_%s_%s" % keys[0], align_bytes=64)
            nc.vector.tensor_copy(
                out=tile[:].rearrange("p n (t m b) -> p n t m b", t=PACK, b=2),
                in_=words.rearrange("p n (m t b) -> p n t m b", t=PACK, b=2),
            )
            for i, key in enumerate(keys):
                operand[key] = tile[:, i, :].bitcast(FP4X4)

        def sort_a_scales(keys, rows):
            tile = keep.tile([P, 2, W], U8, name="a_plane_%s_%s_%s" % keys[0], align_bytes=64)
            nc.vector.tensor_copy(
                out=tile[:].rearrange("p n (t m) -> p n t m", t=PACK),
                in_=rows.rearrange("p n (m t) -> p n t m", t=PACK),
            )
            for i, key in enumerate(keys):
                operand[key + ("scale",)] = tile[:, i, :]

        def open_bank(key, bank):
            banks[key] = psum.tile([P, W], F32, name="bank_%d" % bank)

        def multiply(key, which, order=PASSES):
            e, h, t = key
            nc.tensor.matmul_mx(
                out=banks[key][:],
                lhsT=operand[("a", which, e)][:, t * P : (t + 1) * P],
                lhsT_scale=operand[("a", which, e, "scale")][:, t * P : (t + 1) * P],
                rhs=operand[("v", which, h)],
                rhs_scale=operand[("v", which, h, "scale")],
                start=which == order[0],
                stop=which == order[-1],
            )

        def multiply_pass(e, h, which, order=PASSES):
            for t in range(PACK):
                if which == order[0]:
                    open_bank((e, h, t), e * PACK + t)
                multiply((e, h, t), which, order)

        def multiply_bank(e, h, t):
            open_bank((e, h, t), (e if e < 2 else h) * PACK + t)
            for which in PASSES:
                multiply((e, h, t), which)

        def multiply_block(e, h):
            for t in range(PACK):
                multiply_bank(e, h, t)

        def empty_bank(e, h, t):
            if t == 0:
                flows[(e, h)] = keep.tile([P, PACK, W], F32, name="flow_%d_%d" % (e, h), align_bytes=64)
            nc.scalar.activation(
                out=flows[(e, h)][:, t, :],
                in_=banks[(e, h, t)][:],
                func=IDENTITY,
                bias=source_term[:, t, e : e + 1],
                scale=gain[:, t, e : e + 1],
            )

        def store_flow(e, h, t0, t1):
            rows = out_0[e * W : (e + 1) * W, h * W : (h + 1) * W].rearrange("(p t) m -> p t m", t=PACK)
            nc.sync.dma_start(out=rows[:, t0:t1, :], in_=flows[(e, h)][:, t0:t1, :])

        def empty_block(e, h, step, between=()):
            for t in range(PACK):
                empty_bank(e, h, t)
                if (t + 1) % step == 0:
                    store_flow(e, h, t + 1 - step, t + 1)
                if t == 1:
                    for args in between:
                        store_codes(*args)

        def round_flow(e, h, engine, c0=0, c1=W):
            if e not in rounded:
                rounded[e] = stage.tile([P, PACK * M], BF16, name="rounded", bufs=2, align_bytes=64)
            half = rounded[e][:, h * PACK * W : (h + 1) * PACK * W]
            copy_on(
                engine,
                half.rearrange("p (c i t) -> p c t i", i=4, t=PACK)[:, c0 // 4 : c1 // 4],
                flows[(e, h)][:].rearrange("p t (c i) -> p c t i", i=4)[:, c0 // 4 : c1 // 4],
            )

        def quantize_flow(e, m0, m1):
            if e not in out_codes:
                out_codes[e] = keep.tile([P, M], U32, name="out_codes_%d" % e, align_bytes=64)
            nc.vector.quantize_mx(
                out=out_codes[e][:, m0:m1].bitcast(FP8X4),
                scales=out_planes[PACK * e : P, m0:m1],
                in_=rounded[e][:, PACK * m0 : PACK * m1],
            )

        def store_codes(e, m0, m1):
            words = out_1[e].rearrange("p m t -> p (m t)").bitcast(I32)
            nc.sync.dma_start(out=words[:, m0:m1], in_=out_codes[e][:, m0:m1].bitcast(I32))

        edge_rows = keep.tile([P, W], BF16, align_bytes=64)
        nc.vector.memset(edge_rows[:], 0.0)
        a_scale_rows = []
        for pair in range(2):
            rows_tile = keep.tile([P, INT_PASSES, 2 * W], U8, name="a_scale_rows_%d" % pair, align_bytes=64)
            nc.vector.memset(rows_tile[:].bitcast(I32), 0)
            a_scale_rows.append(rows_tile)
        identity_f32 = keep.tile([P, P], F32, align_bytes=64)
        make_identity(nc, identity_f32[:])
        early_words = [load_a_words(0, 0, 1)]
        load_v(0, 0)
        nc.scalar.dma_start(out=edge_rows[0:GROUPS, :], in_=cond.rearrange("(g w) -> g w", w=W))
        nc.scalar.dma_start(out=edge_rows[GROUPS : 2 * GROUPS, :], in_=emf.rearrange("(g w) -> g w", w=W))
        identity = keep.tile([P, P], BF16, align_bytes=64)
        nc.scalar.activation(out=identity[:], in_=identity_f32[:], func=IDENTITY)
        load_a_scales(0)
        load_v(1, 0)
        early_words.append(load_a_words(0, 1, 2))
        load_v("bnd", 0)
        load_d(0, 1)
        load_d(1, 2)
        for which in PASSES:
            load_v(which, 1)
        late_words = load_a_words(1, 0, 2)
        load_d(2, 4)
        load_a_scales(1)

        gain = keep.tile([P, PACK, GROUPS], F32)
        source_term = keep.tile([P, PACK, GROUPS], F32)
        out_planes = keep.tile([P, M], U8, align_bytes=64)
        turned = psum.tile([P, PACK, P], BF16, name="bank_7")
        for t in range(PACK):
            nc.tensor.transpose(turned[:, t, :], edge_rows[:, t:W:PACK], identity[:])

        def early_codes(g):
            sort_a_codes([("a", g, 0), ("a", g, 1)], early_words[g][:, 0, :].rearrange("p (n w) -> p n w", n=2))

        def early_scales(g):
            sort_a_scales([("a", g, 0), ("a", g, 1)], a_scale_rows[0][:, g, :].rearrange("p (n w) -> p n w", n=2))

        def late_codes(e):
            sort_a_codes([("a", 0, e), ("a", 1, e)], late_words[:, :, (e - 2) * 2 * W : (e - 1) * 2 * W])

        def late_scales(e):
            sort_a_scales([("a", 0, e), ("a", 1, e)], a_scale_rows[1][:, :, (e - 2) * W : (e - 1) * W])

        v00, v10, vb0 = ("v", 0, 0), ("v", 1, 0), ("v", "bnd", 0)
        v01, v11, vb1 = ("v", 0, 1), ("v", 1, 1), ("v", "bnd", 1)
        d0, d1, d2, d3 = [("a", "bnd", e) for e in range(GROUPS)]

        early_codes(0)
        stage_for([v00])
        interleave(v00, "vector", 0, FIRST_SPLIT)
        interleave(v00, "scalar", FIRST_SPLIT, W)
        nc.scalar.copy(out=gain[:], in_=turned[:, :, 0:GROUPS])
        early_scales(0)
        early_scales(1)
        quantize([v00])
        multiply_pass(0, 0, 0)
        nc.vector.tensor_tensor(
            out=source_term[:], in0=turned[:, :, GROUPS : 2 * GROUPS], in1=gain[:], op=mybir.AluOpType.mult
        )
        multiply_pass(1, 0, 0)
        stage_for([v10])
        interleave(v10, "scalar")
        early_codes(1)
        stage_for([vb0])
        interleave(vb0, "vector", 0, BND_SPLIT)
        interleave(vb0, "scalar", BND_SPLIT, W)
        quantize([v10])
        multiply_pass(0, 0, 1)
        multiply_pass(1, 0, 1)
        stage_for([d0])
        interleave(d0, "vector")
        stage_for([d1])
        interleave(d1, "scalar")
        quantize([vb0])
        quantize([d0])
        multiply_pass(0, 0, "bnd")
        stage_for([v01])
        interleave(v01, "scalar", 128, W)
        stage_for([v11])
        interleave(v11, "vector")
        quantize([d1])
        multiply_pass(1, 0, "bnd")
        quantize([v11])
        stage_for([vb1])
        interleave(vb1, "vector")
        interleave(v01, "vector", 0, 128)
        empty_block(0, 0, 2)
        multiply_pass(0, 1, 1, [1, "bnd", 0])
        quantize([vb1])
        multiply_pass(0, 1, "bnd", [1, "bnd", 0])
        quantize([v01])
        multiply_pass(0, 1, 0, [1, "bnd", 0])
        empty_block(1, 0, 2)
        multiply_block(1, 1)
        late_codes(2)
        stage_for([d2])
        interleave(d2, "vector")
        late_scales(2)
        empty_block(0, 1, 2)
        quantize([d2])
        multiply_block(2, 0)
        round_flow(0, 0, "vector")
        round_flow(0, 1, "vector")
        quantize_flow(0, 0, W)
        quantize_flow(0, W, M)
        empty_block(1, 1, 2)
        store_codes(0, 0, W)
        multiply_block(2, 1)
        stage_for([d3])
        interleave(d3, "scalar", 0, LAST_D_SPLIT)
        late_codes(3)
        interleave(d3, "vector", LAST_D_SPLIT, W)
        late_scales(3)
        quantize([d3])
        empty_block(2, 0, 2, [(0, W, M)])
        multiply_block(3, 0)
        round_flow(1, 1, "scalar", W - ROUND_SPLIT, W)
        round_flow(1, 0, "vector")
        round_flow(1, 1, "vector", 0, W - ROUND_SPLIT)
        quantize_flow(1, 0, W)
        quantize_flow(1, W, M)
        empty_block(2, 1, 2)
        store_codes(1, 0, W)
        store_codes(1, W, M)
        multiply_block(3, 1)
        round_flow(2, 1, "scalar", W - ROUND_SPLIT, W)
        round_flow(2, 0, "vector")
        round_flow(2, 1, "vector", 0, W - ROUND_SPLIT)
        quantize_flow(2, 0, W)
        quantize_flow(2, W, M)
        empty_block(3, 0, 2)
        store_codes(2, 0, W)
        round_flow(3, 0, "vector")
        empty_block(3, 1, 2, [(2, W, M)])
        round_flow(3, 1, "scalar", W - TAIL_SPLIT, W)
        round_flow(3, 1, "vector", 0, W - TAIL_SPLIT)
        quantize_flow(3, 0, W)
        store_codes(3, 0, W)
        quantize_flow(3, W, M)
        store_codes(3, W, M)

        for q in range(4):
            nc.scalar.dma_start(
                out=out_2.bitcast(I32)[:, 4 * q : 4 * q + 4, :],
                in_=out_planes[32 * q : 32 * q + 16, :].bitcast(I32),
            )
